import numpy as np
import ml_dtypes


def mxq(x, axis, fmt="e4m3"):
    dtype, down = {"e4m3": (ml_dtypes.float8_e4m3fn, 7), "e5m2": (ml_dtypes.float8_e5m2, 14)}[fmt]
    v = np.moveaxis(np.asarray(x, np.float32).astype(ml_dtypes.bfloat16).astype(np.float64), axis, -1)
    blocks = v.reshape(v.shape[:-1] + (-1, 32))
    amax = np.abs(blocks).max(-1, keepdims=True)
    byte = np.maximum(np.where(amax > 0, np.frexp(amax)[1] - 1 + 127, 0) - down, 1)
    scale = np.exp2(byte - 127.0)
    codes = (blocks / scale).astype(np.float32).astype(dtype).astype(np.float64)
    return np.moveaxis((codes * scale).reshape(v.shape), -1, axis)


WIDE = False


def mx_kscale(k):
    if not WIDE:
        return np.ones(k)
    levels = np.array([10, -10, 5, -5, 0])
    if k % 512:
        return np.exp2(np.random.permutation(np.resize(levels, k // 32))).repeat(32)
    a = np.empty((k // 512, 16))
    for p in range(k // 512):
        a[p, :8] = np.random.permutation(np.resize(levels, 8))
        for g in range(8):
            far = levels[np.abs(levels - a[p, g]) >= 10]
            a[p, g + 8] = far[np.random.randint(len(far))]
    return np.exp2(a.ravel()).repeat(32)


def f64(x):
    return np.asarray(x).astype(np.float64)


def striped(idx):
    return np.tile(idx.reshape(-1, 16).T, (8, 1)).astype(np.uint16)


def unstriped(offs):
    return offs[:16].T.reshape(-1).astype(np.int64)


def pack_weight(w):
    k, n = w.shape
    w = f64(np.asarray(w, np.float32).astype(ml_dtypes.bfloat16)).reshape(k // 32, 32, n)
    amax = np.abs(w).max(1)
    byte = np.clip(np.where(amax > 0, np.frexp(amax)[1] - 1 + 127 - 7, 1), 1, 254)
    scaled = (w * np.exp2(127.0 - byte)[:, None, :]).reshape(k, n).astype(np.float32)
    words = np.ascontiguousarray(scaled.reshape(k // 512, 128, 4, n).transpose(0, 1, 3, 2)).astype(ml_dtypes.float8_e4m3fn).view(np.uint8)
    return words, np.ascontiguousarray(byte.astype(np.uint8).reshape(k // 512, 16, n))


def unpack_weight(words, scales):
    g, p, n, _ = words.shape
    vals = np.ascontiguousarray(words).view(ml_dtypes.float8_e4m3fn).astype(np.float64) * np.repeat(np.exp2(scales.astype(np.float64) - 127.0), 8, axis=1)[..., None]
    return vals.transpose(0, 1, 3, 2).reshape(g * 512, n)


def silu(v):
    return v / (1.0 + np.exp(-np.maximum(v, -700.0)))


K, T, E, C, N = 1536, 1024, 16, 128, 128


def by_expert(wq, xq):
    return np.concatenate([wq[e].T @ xq[:, e * C:(e + 1) * C] for e in range(E)], axis=1)


def setup_inputs():
    n = np.random.standard_normal
    s = mx_kscale(K)[:, None]
    first = np.random.permutation(np.repeat(np.arange(E), T // E))
    second = (first + 1 + np.random.permutation(np.repeat(np.arange(E - 1), -(-T // (E - 1)))[:T])) % E
    while np.bincount(second, minlength=E).max() != T // E:
        load = np.bincount(second, minlength=E); hi, lo = int(load.argmax()), int(load.argmin())
        t = np.flatnonzero((second == hi) & (first != lo))[0]; second[t] = lo
    slot_token = np.empty(E * C, np.int64); pos = np.empty((2, T), np.int64); fill = np.zeros(E, np.int64)
    place = np.stack([np.random.permutation(C) for _ in range(E)])
    for r, deal in enumerate((first, second)):
        for t in np.random.permutation(T):
            e = deal[t]; j = e * C + place[e, fill[e]]; fill[e] += 1; slot_token[j] = t; pos[r, t] = j
    g = np.random.uniform(0.2, 0.8, T)
    packed = [pack_weight(m) for m in n((E, K, N)) / np.sqrt(K) / s[None]]
    return {
        "xT": (n((K, T)) * s).astype(np.float32),
        "w_words": np.stack([m[0] for m in packed]),
        "w_scales": np.stack([m[1] for m in packed]),
        "b": (0.3 * n((N, E))).astype(np.float32),
        "gate": np.stack([np.tile(g, (N, 1)), np.tile(1.0 - g, (N, 1))]).astype(np.float32),
        "offs": striped(slot_token),
        "pos1": striped(pos[0]),
        "pos2": striped(pos[1]),
    }


def reference(xT, w_words, w_scales, b, gate, offs, pos1, pos2):
    idx = unstriped(offs)
    xq = mxq(f64(xT)[:, idx], 0, "e4m3")
    w = np.stack([unpack_weight(w_words[e], w_scales[e]) for e in range(E)])
    y = by_expert(w, xq)
    y = silu(y + np.repeat(f64(b), C, axis=1))
    return f64(gate[0]) * y[:, unstriped(pos1)] + f64(gate[1]) * y[:, unstriped(pos2)]

@@ -1,0 +1,161 @@
+from contextlib import ExitStack
+
+import concourse.mybir as mybir
+
+F32 = mybir.dt.float32
+BF16 = mybir.dt.bfloat16
+I32 = mybir.dt.int32
+U32 = mybir.dt.uint32
+U16 = mybir.dt.uint16
+U8 = mybir.dt.uint8
+FP8X4 = mybir.dt.float8_e4m3fn_x4
+MULT = mybir.AluOpType.mult
+ADD = mybir.AluOpType.add
+SILU = mybir.ActivationFunctionType.Silu
+
+P = 128
+K, T, E, C = 1536, 1024, 16, 128
+SLOTS = E * C
+PASSES = 3
+FLOPS = 2 * K * P * SLOTS
+
+LOADS = [[(0, 512), (512, 256), (768, 256)], [(0, 256), (256, 256), (512, 256), (768, 256)], [(0, 512), (512, 512)]]
+
+
+def offs_slice(tile, lo, n):
+    return tile[:, lo // 16 : (lo + n) // 16]
+
+
+def interleave(engine_copy, dst, src):
+    engine_copy(out=dst.rearrange("p (c i) t -> p c t i", i=4), in_=src.rearrange("p t (c i) -> p c t i", i=4))
+
+
+def tile_routed_moe_kernel(tc, xT, w_words, w_scales, b, gate, offs, pos1, pos2, out):
+    nc = tc.nc
+    with ExitStack() as ctx:
+        keep = ctx.enter_context(tc.tile_pool(name="keep", bufs=1))
+        psum = ctx.enter_context(tc.psum_pool(name="psum", bufs=8))
+
+        offs_t = keep.tile([P, SLOTS // 16], U16, name="offs_t")
+        pos1_t = keep.tile([P, T // 16], U16, name="pos1_t")
+        pos2_t = keep.tile([P, T // 16], U16, name="pos2_t")
+        bias = keep.tile([P, E], F32, name="bias")
+        gates = [keep.tile([P, T], F32, name=f"gate{r}") for r in range(2)]
+        w_codes = keep.tile([P, E * PASSES, C], U32, name="w_codes", align_bytes=64)
+        w_sc = keep.tile([P, E, C], U8, name="w_sc", align_bytes=64)
+        x_codes = [keep.tile([P, T], U32, name=f"x_codes{a}", align_bytes=64) for a in range(PASSES)]
+        x_sc = keep.tile([P, T], U8, name="x_sc", align_bytes=64)
+        g_codes = [keep.tile([P, SLOTS], U32, name=f"g_codes{a}", align_bytes=64) for a in range(PASSES)]
+        g_sc = keep.tile([P, SLOTS], U8, name="g_sc", align_bytes=64)
+        y = keep.tile([P, SLOTS], F32, name="y")
+        warm = keep.tile([P, 1], F32, name="warm")
+        warm2 = keep.tile([P, 1], F32, name="warm2")
+
+        nc.gpsimd.memset(warm[:], 0.0)
+        nc.scalar.activation(out=warm2[:], in_=warm[:], func=SILU)
+        nc.gpsimd.memset(x_sc[:], 0)
+        nc.gpsimd.memset(w_sc[:].rearrange("p e n -> p (e n)").bitcast(I32), 0)
+
+        x_view = xT.rearrange("(g p t) n -> g p t n", p=P, t=4)
+        raws = [[], [], []]
+        for a in range(PASSES):
+            for i, (lo, n) in enumerate(LOADS[a]):
+                raw = keep.tile([P, 4, n], F32, name=f"raw{a}_{i}")
+                nc.sync.dma_start(out=raw[:], in_=x_view[a, :, :, lo : lo + n])
+                raws[a].append(raw)
+                if a == 0 and i == 0:
+                    nc.sync.dma_start(out=offs_t[:], in_=offs)
+        nc.sync.dma_start(out=bias[:], in_=b)
+        for a in range(PASSES):
+            for q in range(4):
+                r0 = 32 * q + 4 * a
+                nc.sync.dma_start(
+                    out=w_sc[r0 : r0 + 4, :, :].bitcast(I32),
+                    in_=w_scales[:, a, 4 * q : 4 * q + 4, :].rearrange("e q n -> q e n").bitcast(I32),
+                )
+        for e0 in range(0, E, 4):
+            nc.sync.dma_start(
+                out=w_codes[:, e0 * PASSES : (e0 + 4) * PASSES, :].bitcast(I32),
+                in_=w_words[e0 : e0 + 4].rearrange("e a p n r -> p (e a) (n r)").bitcast(I32),
+            )
+        nc.sync.dma_start(out=pos1_t[:], in_=pos1)
+        nc.sync.dma_start(out=pos2_t[:], in_=pos2)
+        for r in range(2):
+            nc.sync.dma_start(out=gates[r][:], in_=gate[r])
+
+        def grouped_tile(n, a, lo):
+            return keep.tile([P, n, 4], BF16, name=f"grp{a}_{lo}", align_bytes=64)
+
+        def quantize(a, lo, grp):
+            n = grp.shape[1]
+            nc.vector.quantize_mx(
+                out=x_codes[a][:, lo : lo + n].bitcast(FP8X4),
+                scales=x_sc[4 * a : P, lo : lo + n],
+                in_=grp[:].rearrange("p w j -> p (w j)"),
+            )
+
+        def gather_words(a, lo, n):
+            nc.vector.tensor_copy(g_codes[a][:, lo : lo + n], x_codes[a][:].indirect(offs_slice(offs_t, lo, n)))
+
+        def gather_scales(lo, n):
+            nc.vector.tensor_copy(g_sc[:, lo : lo + n], x_sc[:].indirect(offs_slice(offs_t, lo, n)))
+
+        g00, g01, g02, g03 = [grouped_tile(256, 0, lo) for lo in (0, 256, 512, 768)]
+        interleave(nc.vector.tensor_copy, g00[:], raws[0][0][:, :, 0:256])
+        interleave(nc.scalar.copy, g01[:], raws[0][0][:, :, 256:512])
+        interleave(nc.vector.tensor_copy, g02[:], raws[0][1][:])
+        quantize(0, 0, g00)
+        quantize(0, 256, g01)
+        interleave(nc.scalar.copy, g03[:, 160:256, :], raws[0][2][:, :, 160:256])
+        interleave(nc.vector.tensor_copy, g03[:, 0:160, :], raws[0][2][:, :, 0:160])
+        quantize(0, 512, g02)
+        quantize(0, 768, g03)
+
+        for lo, n in ((0, 768), (768, 768), (1536, 512)):
+            gather_words(0, lo, n)
+
+        for a in (1, 2):
+            grps = []
+            for i, (lo, n) in enumerate(LOADS[a]):
+                grp = grouped_tile(n, a, lo)
+                interleave(nc.scalar.copy, grp[:], raws[a][i][:])
+                grps.append((lo, grp))
+            for lo, grp in grps:
+                quantize(a, lo, grp)
+            if a == 1:
+                for lo, n in ((0, 768), (768, 768), (1536, 512)):
+                    gather_words(1, lo, n)
+
+        def expert(e):
+            acc = psum.tile([P, 512], F32, name="acc")
+            cols = slice(e * C, (e + 1) * C)
+            for a in range(PASSES):
+                nc.tensor.matmul_mx(
+                    out=acc[:, 0:C],
+                    lhsT=w_codes[:, e * PASSES + a, :].bitcast(FP8X4),
+                    lhsT_scale=w_sc[4 * a : P, e, :],
+                    rhs=g_codes[a][:, cols].bitcast(FP8X4),
+                    rhs_scale=g_sc[4 * a : P, cols],
+                    start=(a == 0),
+                    stop=(a == PASSES - 1),
+                )
+            nc.scalar.activation(out=y[:, cols], in_=acc[:, 0:C], func=SILU, bias=bias[:, e : e + 1])
+
+        scale_cuts = [(0, 768), (768, 768), (1536, 512)]
+        word_cuts = [(0, 512), (512, 512), (1024, 512), (1536, 384), (1920, 128)]
+        for i, (lo, n) in enumerate(word_cuts):
+            if i < len(scale_cuts):
+                gather_scales(*scale_cuts[i])
+            gather_words(2, lo, n)
+            for e in range(lo // C, (lo + n) // C):
+                expert(e)
+
+        m1 = keep.tile([P, T], F32, name="m1")
+        m2 = keep.tile([P, T], F32, name="m2")
+        res = keep.tile([P, T], F32, name="res")
+        nc.vector.tensor_tensor(m1[:], y[:].indirect(pos1_t[:]), gates[0][:], MULT)
+        for lo, n in ((0, 640), (640, 384)):
+            cols = slice(lo, lo + n)
+            nc.vector.tensor_tensor(m2[:, cols], y[:].indirect(offs_slice(pos2_t, lo, n)), gates[1][:, cols], MULT)
+            nc.vector.tensor_tensor(res[:, cols], m1[:, cols], m2[:, cols], ADD)
+            nc.sync.dma_start(out=out[:, cols], in_=res[:, cols])

@@ -19,7 +19,7 @@ SLOTS = E * C
 PASSES = 3
 FLOPS = 2 * K * P * SLOTS
 
-LOADS = [[(0, 512), (512, 256), (768, 256)], [(0, 256), (256, 256), (512, 256), (768, 256)], [(0, 512), (512, 512)]]
+LOADS = [[(0, 512), (512, 256), (768, 256)], [(0, 512), (512, 512)], [(0, 512), (512, 512)]]
 
 
 def offs_slice(tile, lo, n):
@@ -42,7 +42,7 @@ def tile_routed_moe_kernel(tc, xT, w_words, w_scales, b, gate, offs, pos1, pos2,
         bias = keep.tile([P, E], F32, name="bias")
         gates = [keep.tile([P, T], F32, name=f"gate{r}") for r in range(2)]
         w_codes = keep.tile([P, E * PASSES, C], U32, name="w_codes", align_bytes=64)
-        w_sc = keep.tile([P, E, C], U8, name="w_sc", align_bytes=64)
+        w_sc = keep.tile([P, E * PASSES, C], U8, name="w_sc", align_bytes=64)
         x_codes = [keep.tile([P, T], U32, name=f"x_codes{a}", align_bytes=64) for a in range(PASSES)]
         x_sc = keep.tile([P, T], U8, name="x_sc", align_bytes=64)
         g_codes = [keep.tile([P, SLOTS], U32, name=f"g_codes{a}", align_bytes=64) for a in range(PASSES)]
@@ -54,34 +54,54 @@ def tile_routed_moe_kernel(tc, xT, w_words, w_scales, b, gate, offs, pos1, pos2,
         nc.gpsimd.memset(warm[:], 0.0)
         nc.scalar.activation(out=warm2[:], in_=warm[:], func=SILU)
         nc.gpsimd.memset(x_sc[:], 0)
-        nc.gpsimd.memset(w_sc[:].rearrange("p e n -> p (e n)").bitcast(I32), 0)
+        nc.vector.memset(w_sc[:].rearrange("p e n -> p (e n)").bitcast(I32), 0)
 
         x_view = xT.rearrange("(g p t) n -> g p t n", p=P, t=4)
         raws = [[], [], []]
-        for a in range(PASSES):
-            for i, (lo, n) in enumerate(LOADS[a]):
-                raw = keep.tile([P, 4, n], F32, name=f"raw{a}_{i}")
-                nc.sync.dma_start(out=raw[:], in_=x_view[a, :, :, lo : lo + n])
-                raws[a].append(raw)
-                if a == 0 and i == 0:
-                    nc.sync.dma_start(out=offs_t[:], in_=offs)
-        nc.sync.dma_start(out=bias[:], in_=b)
-        for a in range(PASSES):
-            for q in range(4):
-                r0 = 32 * q + 4 * a
+
+        def load_x(a, i):
+            lo, n = LOADS[a][i]
+            raw = keep.tile([P, 4, n], F32, name=f"raw{a}_{i}")
+            nc.sync.dma_start(out=raw[:], in_=x_view[a, :, :, lo : lo + n])
+            raws[a].append(raw)
+
+        def load_scale_rows(q0, n):
+            for q in range(q0, q0 + n):
+                row = 32 * (q // 4) + q % 4
                 nc.sync.dma_start(
-                    out=w_sc[r0 : r0 + 4, :, :].bitcast(I32),
-                    in_=w_scales[:, a, 4 * q : 4 * q + 4, :].rearrange("e q n -> q e n").bitcast(I32),
+                    out=w_sc[row : row + 1, :, :].bitcast(I32),
+                    in_=w_scales[:, :, q : q + 1, :].rearrange("e a q n -> q (e a) n").bitcast(I32),
                 )
-        for e0 in range(0, E, 4):
+
+        def load_words(e0, n):
             nc.sync.dma_start(
-                out=w_codes[:, e0 * PASSES : (e0 + 4) * PASSES, :].bitcast(I32),
-                in_=w_words[e0 : e0 + 4].rearrange("e a p n r -> p (e a) (n r)").bitcast(I32),
+                out=w_codes[:, e0 * PASSES : (e0 + n) * PASSES, :].bitcast(I32),
+                in_=w_words[e0 : e0 + n].rearrange("e a p n r -> p (e a) (n r)").bitcast(I32),
             )
+
+        load_x(0, 0)
+        load_x(0, 1)
+        load_x(0, 2)
+        nc.sync.dma_start(out=offs_t[:], in_=offs)
+        nc.sync.dma_start(out=bias[:], in_=b)
+        load_scale_rows(0, 2)
+        load_x(1, 0)
+        load_scale_rows(2, 2)
+        load_x(1, 1)
+        load_scale_rows(4, 3)
+        load_x(2, 0)
+        load_scale_rows(7, 3)
+        load_x(2, 1)
+        load_scale_rows(10, 3)
+        load_words(0, 4)
+        load_scale_rows(13, 3)
+        load_words(4, 4)
+        load_words(8, 4)
         nc.sync.dma_start(out=pos1_t[:], in_=pos1)
+        load_words(12, 4)
+        nc.sync.dma_start(out=gates[0][:], in_=gate[0])
         nc.sync.dma_start(out=pos2_t[:], in_=pos2)
-        for r in range(2):
-            nc.sync.dma_start(out=gates[r][:], in_=gate[r])
+        nc.sync.dma_start(out=gates[1][:], in_=gate[1])
 
         def grouped_tile(n, a, lo):
             return keep.tile([P, n, 4], BF16, name=f"grp{a}_{lo}", align_bytes=64)
@@ -100,31 +120,24 @@ def tile_routed_moe_kernel(tc, xT, w_words, w_scales, b, gate, offs, pos1, pos2,
         def gather_scales(lo, n):
             nc.vector.tensor_copy(g_sc[:, lo : lo + n], x_sc[:].indirect(offs_slice(offs_t, lo, n)))
 
-        g00, g01, g02, g03 = [grouped_tile(256, 0, lo) for lo in (0, 256, 512, 768)]
-        interleave(nc.vector.tensor_copy, g00[:], raws[0][0][:, :, 0:256])
-        interleave(nc.scalar.copy, g01[:], raws[0][0][:, :, 256:512])
-        interleave(nc.vector.tensor_copy, g02[:], raws[0][1][:])
-        quantize(0, 0, g00)
-        quantize(0, 256, g01)
-        interleave(nc.scalar.copy, g03[:, 160:256, :], raws[0][2][:, :, 160:256])
-        interleave(nc.vector.tensor_copy, g03[:, 0:160, :], raws[0][2][:, :, 0:160])
-        quantize(0, 512, g02)
-        quantize(0, 768, g03)
-
-        for lo, n in ((0, 768), (768, 768), (1536, 512)):
-            gather_words(0, lo, n)
-
-        for a in (1, 2):
+        VEC, SCA = nc.vector.tensor_copy, nc.scalar.copy
+        SPLIT = [[256, 256, 160], [0, 128], [0, 0]]
+        for a in range(PASSES):
             grps = []
             for i, (lo, n) in enumerate(LOADS[a]):
                 grp = grouped_tile(n, a, lo)
-                interleave(nc.scalar.copy, grp[:], raws[a][i][:])
+                v = SPLIT[a][i]
+                if v < n:
+                    interleave(SCA, grp[:, v:n, :], raws[a][i][:, :, v:n])
+                if v:
+                    interleave(VEC, grp[:, 0:v, :], raws[a][i][:, :, 0:v])
                 grps.append((lo, grp))
-            for lo, grp in grps:
-                quantize(a, lo, grp)
-            if a == 1:
+                if i:
+                    quantize(a, *grps[i - 1])
+            quantize(a, *grps[-1])
+            if a < 2:
                 for lo, n in ((0, 768), (768, 768), (1536, 512)):
-                    gather_words(1, lo, n)
+                    gather_words(a, lo, n)
 
         def expert(e):
             acc = psum.tile([P, 512], F32, name="acc")
@@ -133,7 +146,7 @@ def tile_routed_moe_kernel(tc, xT, w_words, w_scales, b, gate, offs, pos1, pos2,
                 nc.tensor.matmul_mx(
                     out=acc[:, 0:C],
                     lhsT=w_codes[:, e * PASSES + a, :].bitcast(FP8X4),
-                    lhsT_scale=w_sc[4 * a : P, e, :],
+                    lhsT_scale=w_sc[:, e * PASSES + a, :],
                     rhs=g_codes[a][:, cols].bitcast(FP8X4),
                     rhs_scale=g_sc[4 * a : P, cols],
                     start=(a == 0),
@@ -141,11 +154,10 @@ def tile_routed_moe_kernel(tc, xT, w_words, w_scales, b, gate, offs, pos1, pos2,
                 )
             nc.scalar.activation(out=y[:, cols], in_=acc[:, 0:C], func=SILU, bias=bias[:, e : e + 1])
 
-        scale_cuts = [(0, 768), (768, 768), (1536, 512)]
-        word_cuts = [(0, 512), (512, 512), (1024, 512), (1536, 384), (1920, 128)]
-        for i, (lo, n) in enumerate(word_cuts):
-            if i < len(scale_cuts):
-                gather_scales(*scale_cuts[i])
+        scale_cuts = {0: (0, 768), 512: (768, 768), 1024: (1536, 512)}
+        for lo, n in [(0, 512), (512, 512), (1024, 512), (1536, 384), (1920, 128)]:
+            if lo in scale_cuts:
+                gather_scales(*scale_cuts[lo])
             gather_words(2, lo, n)
             for e in range(lo // C, (lo + n) // C):
                 expert(e)
@@ -154,7 +166,7 @@ def tile_routed_moe_kernel(tc, xT, w_words, w_scales, b, gate, offs, pos1, pos2,
         m2 = keep.tile([P, T], F32, name="m2")
         res = keep.tile([P, T], F32, name="res")
         nc.vector.tensor_tensor(m1[:], y[:].indirect(pos1_t[:]), gates[0][:], MULT)
-        for lo, n in ((0, 640), (640, 384)):
+        for lo, n in ((0, 768), (768, 256)):
             cols = slice(lo, lo + n)
             nc.vector.tensor_tensor(m2[:, cols], y[:].indirect(offs_slice(pos2_t, lo, n)), gates[1][:, cols], MULT)
             nc.vector.tensor_tensor(res[:, cols], m1[:, cols], m2[:, cols], ADD)

@@ -19,7 +19,7 @@ SLOTS = E * C
 PASSES = 3
 FLOPS = 2 * K * P * SLOTS
 
-LOADS = [[(0, 512), (512, 256), (768, 256)], [(0, 512), (512, 512)], [(0, 512), (512, 512)]]
+LOADS = [[(0, 512), (512, 256), (768, 256)], [(0, 256), (256, 256), (512, 256), (768, 256)], [(0, 256), (256, 256), (512, 256), (768, 256)]]
 
 
 def offs_slice(tile, lo, n):
@@ -34,6 +34,7 @@ def tile_routed_moe_kernel(tc, xT, w_words, w_scales, b, gate, offs, pos1, pos2,
     nc = tc.nc
     with ExitStack() as ctx:
         keep = ctx.enter_context(tc.tile_pool(name="keep", bufs=1))
+        ring = ctx.enter_context(tc.tile_pool(name="ring", bufs=1))
         psum = ctx.enter_context(tc.psum_pool(name="psum", bufs=8))
 
         offs_t = keep.tile([P, SLOTS // 16], U16, name="offs_t")
@@ -43,7 +44,6 @@ def tile_routed_moe_kernel(tc, xT, w_words, w_scales, b, gate, offs, pos1, pos2,
         gates = [keep.tile([P, T], F32, name=f"gate{r}") for r in range(2)]
         w_codes = keep.tile([P, E * PASSES, C], U32, name="w_codes", align_bytes=64)
         w_sc = keep.tile([P, E * PASSES, C], U8, name="w_sc", align_bytes=64)
-        x_codes = [keep.tile([P, T], U32, name=f"x_codes{a}", align_bytes=64) for a in range(PASSES)]
         x_sc = keep.tile([P, T], U8, name="x_sc", align_bytes=64)
         g_codes = [keep.tile([P, SLOTS], U32, name=f"g_codes{a}", align_bytes=64) for a in range(PASSES)]
         g_sc = keep.tile([P, SLOTS], U8, name="g_sc", align_bytes=64)
@@ -81,30 +81,26 @@ def tile_routed_moe_kernel(tc, xT, w_words, w_scales, b, gate, offs, pos1, pos2,
 
         load_x(0, 0)
         load_x(0, 1)
-        load_x(0, 2)
         nc.sync.dma_start(out=offs_t[:], in_=offs)
+        load_x(0, 2)
         nc.sync.dma_start(out=bias[:], in_=b)
-        load_scale_rows(0, 2)
         load_x(1, 0)
-        load_scale_rows(2, 2)
-        load_x(1, 1)
-        load_scale_rows(4, 3)
-        load_x(2, 0)
-        load_scale_rows(7, 3)
-        load_x(2, 1)
-        load_scale_rows(10, 3)
+        for i in range(1, 4):
+            load_x(1, i)
+            load_scale_rows(i - 1, 1)
+        for i in range(4):
+            load_x(2, i)
+            load_scale_rows(3 + 2 * i, 2)
         load_words(0, 4)
-        load_scale_rows(13, 3)
+        load_scale_rows(11, 3)
         load_words(4, 4)
+        load_scale_rows(14, 2)
         load_words(8, 4)
         nc.sync.dma_start(out=pos1_t[:], in_=pos1)
         load_words(12, 4)
         nc.sync.dma_start(out=gates[0][:], in_=gate[0])
         nc.sync.dma_start(out=pos2_t[:], in_=pos2)
         nc.sync.dma_start(out=gates[1][:], in_=gate[1])
-
-        def grouped_tile(n, a, lo):
-            return keep.tile([P, n, 4], BF16, name=f"grp{a}_{lo}", align_bytes=64)
 
         def quantize(a, lo, grp):
             n = grp.shape[1]
@@ -121,30 +117,53 @@ def tile_routed_moe_kernel(tc, xT, w_words, w_scales, b, gate, offs, pos1, pos2,
             nc.vector.tensor_copy(g_sc[:, lo : lo + n], x_sc[:].indirect(offs_slice(offs_t, lo, n)))
 
         VEC, SCA = nc.vector.tensor_copy, nc.scalar.copy
-        SPLIT = [[256, 256, 160], [0, 128], [0, 0]]
-        for a in range(PASSES):
-            grps = []
-            for i, (lo, n) in enumerate(LOADS[a]):
-                grp = grouped_tile(n, a, lo)
-                v = SPLIT[a][i]
-                if v < n:
-                    interleave(SCA, grp[:, v:n, :], raws[a][i][:, :, v:n])
-                if v:
-                    interleave(VEC, grp[:, 0:v, :], raws[a][i][:, :, 0:v])
-                grps.append((lo, grp))
-                if i:
-                    quantize(a, *grps[i - 1])
-            quantize(a, *grps[-1])
-            if a < 2:
+        x_codes = []
+
+        def new_codes(a):
+            x_codes.append(ring.tile([P, T], U32, name=f"x_codes{a}", tag="x_codes", align_bytes=64))
+
+        new_codes(0)
+        grp = [keep.tile([P, 256, 4], BF16, name=f"grp0_{i}", align_bytes=64) for i in range(4)]
+        interleave(VEC, grp[0][:], raws[0][0][:, :, 0:256])
+        interleave(SCA, grp[1][:], raws[0][0][:, :, 256:512])
+        interleave(VEC, grp[2][:], raws[0][1][:])
+        quantize(0, 0, grp[0])
+        quantize(0, 256, grp[1])
+        interleave(SCA, grp[3][:, 160:256, :], raws[0][2][:, :, 160:256])
+        interleave(VEC, grp[3][:, 0:160, :], raws[0][2][:, :, 0:160])
+        quantize(0, 512, grp[2])
+        quantize(0, 768, grp[3])
+        for lo, n in ((0, 768), (768, 768), (1536, 512)):
+            gather_words(0, lo, n)
+
+        for a in (1, 2):
+            new_codes(a)
+            first = ring.tile([P, 512, 4], BF16, name=f"grp{a}_first", tag=f"grp{a}", align_bytes=64)
+            third = keep.tile([P, 256, 4], BF16, name=f"grp{a}_third", align_bytes=64)
+            last_s = keep.tile([P, 128, 4], BF16, name=f"grp{a}_s", align_bytes=64)
+            interleave(SCA, first[:, 0:256, :], raws[a][0][:])
+            interleave(SCA, first[:, 256:512, :], raws[a][1][:])
+            interleave(SCA, third[:], raws[a][2][:])
+            interleave(SCA, last_s[:], raws[a][3][:, :, 128:256])
+            quantize(a, 0, first)
+            last_v = ring.tile([P, 128, 4], BF16, name=f"grp{a}_v", tag=f"grp{a}", align_bytes=64)
+            interleave(VEC, last_v[:], raws[a][3][:, :, 0:128])
+            quantize(a, 512, third)
+            quantize(a, 768, last_v)
+            quantize(a, 896, last_s)
+            if a == 1:
                 for lo, n in ((0, 768), (768, 768), (1536, 512)):
                     gather_words(a, lo, n)
 
-        def expert(e):
-            acc = psum.tile([P, 512], F32, name="acc")
+        accs = {}
+
+        def multiply(e, passes):
+            if e not in accs:
+                accs[e] = psum.tile([P, 512], F32, name="acc")
             cols = slice(e * C, (e + 1) * C)
-            for a in range(PASSES):
+            for a in passes:
                 nc.tensor.matmul_mx(
-                    out=acc[:, 0:C],
+                    out=accs[e][:, 0:C],
                     lhsT=w_codes[:, e * PASSES + a, :].bitcast(FP8X4),
                     lhsT_scale=w_sc[:, e * PASSES + a, :],
                     rhs=g_codes[a][:, cols].bitcast(FP8X4),
@@ -152,22 +171,35 @@ def tile_routed_moe_kernel(tc, xT, w_words, w_scales, b, gate, offs, pos1, pos2,
                     start=(a == 0),
                     stop=(a == PASSES - 1),
                 )
-            nc.scalar.activation(out=y[:, cols], in_=acc[:, 0:C], func=SILU, bias=bias[:, e : e + 1])
 
-        scale_cuts = {0: (0, 768), 512: (768, 768), 1024: (1536, 512)}
-        for lo, n in [(0, 512), (512, 512), (1024, 512), (1536, 384), (1920, 128)]:
-            if lo in scale_cuts:
-                gather_scales(*scale_cuts[lo])
+        def finish(e):
+            cols = slice(e * C, (e + 1) * C)
+            nc.scalar.activation(out=y[:, cols], in_=accs[e][:, 0:C], func=SILU, bias=bias[:, e : e + 1])
+
+        for lo in (0, 768):
+            gather_scales(lo, 768)
+            gather_words(2, lo, 768)
+            for e in range(lo // C, (lo + 768) // C):
+                multiply(e, (0, 1, 2))
+                finish(e)
+        gather_scales(1536, 512)
+        for e in range(12, 16):
+            multiply(e, (0, 1))
+        for lo, n in ((1536, 384), (1920, 128)):
             gather_words(2, lo, n)
             for e in range(lo // C, (lo + n) // C):
-                expert(e)
+                multiply(e, (2,))
+                finish(e)
 
         m1 = keep.tile([P, T], F32, name="m1")
         m2 = keep.tile([P, T], F32, name="m2")
         res = keep.tile([P, T], F32, name="res")
+        halves = ((0, 512), (512, 512))
         nc.vector.tensor_tensor(m1[:], y[:].indirect(pos1_t[:]), gates[0][:], MULT)
-        for lo, n in ((0, 768), (768, 256)):
+        for lo, n in halves:
             cols = slice(lo, lo + n)
             nc.vector.tensor_tensor(m2[:, cols], y[:].indirect(offs_slice(pos2_t, lo, n)), gates[1][:, cols], MULT)
+        for lo, n in halves:
+            cols = slice(lo, lo + n)
             nc.vector.tensor_tensor(res[:, cols], m1[:, cols], m2[:, cols], ADD)
             nc.sync.dma_start(out=out[:, cols], in_=res[:, cols])

@@ -34,7 +34,6 @@ def tile_routed_moe_kernel(tc, xT, w_words, w_scales, b, gate, offs, pos1, pos2,
     nc = tc.nc
     with ExitStack() as ctx:
         keep = ctx.enter_context(tc.tile_pool(name="keep", bufs=1))
-        ring = ctx.enter_context(tc.tile_pool(name="ring", bufs=1))
         psum = ctx.enter_context(tc.psum_pool(name="psum", bufs=8))
 
         offs_t = keep.tile([P, SLOTS // 16], U16, name="offs_t")
@@ -43,7 +42,7 @@ def tile_routed_moe_kernel(tc, xT, w_words, w_scales, b, gate, offs, pos1, pos2,
         bias = keep.tile([P, E], F32, name="bias")
         gates = [keep.tile([P, T], F32, name=f"gate{r}") for r in range(2)]
         w_codes = keep.tile([P, E * PASSES, C], U32, name="w_codes", align_bytes=64)
-        w_sc = keep.tile([P, E * PASSES, C], U8, name="w_sc", align_bytes=64)
+        w_sc = keep.tile([P, E, C], U8, name="w_sc", align_bytes=64)
         x_sc = keep.tile([P, T], U8, name="x_sc", align_bytes=64)
         g_codes = [keep.tile([P, SLOTS], U32, name=f"g_codes{a}", align_bytes=64) for a in range(PASSES)]
         g_sc = keep.tile([P, SLOTS], U8, name="g_sc", align_bytes=64)
@@ -54,7 +53,7 @@ def tile_routed_moe_kernel(tc, xT, w_words, w_scales, b, gate, offs, pos1, pos2,
         nc.gpsimd.memset(warm[:], 0.0)
         nc.scalar.activation(out=warm2[:], in_=warm[:], func=SILU)
         nc.gpsimd.memset(x_sc[:], 0)
-        nc.vector.memset(w_sc[:].rearrange("p e n -> p (e n)").bitcast(I32), 0)
+        nc.gpsimd.memset(w_sc[:].rearrange("p e n -> p (e n)").bitcast(I32), 0)
 
         x_view = xT.rearrange("(g p t) n -> g p t n", p=P, t=4)
         raws = [[], [], []]
@@ -65,12 +64,12 @@ def tile_routed_moe_kernel(tc, xT, w_words, w_scales, b, gate, offs, pos1, pos2,
             nc.sync.dma_start(out=raw[:], in_=x_view[a, :, :, lo : lo + n])
             raws[a].append(raw)
 
-        def load_scale_rows(q0, n):
-            for q in range(q0, q0 + n):
-                row = 32 * (q // 4) + q % 4
+        def load_scales(first, n):
+            for a, q in [divmod(j, 4) for j in range(first, first + n)]:
+                row = 32 * q + 4 * a
                 nc.sync.dma_start(
-                    out=w_sc[row : row + 1, :, :].bitcast(I32),
-                    in_=w_scales[:, :, q : q + 1, :].rearrange("e a q n -> q (e a) n").bitcast(I32),
+                    out=w_sc[row : row + 4, :, :].bitcast(I32),
+                    in_=w_scales[:, a, 4 * q : 4 * q + 4, :].rearrange("e q n -> q e n").bitcast(I32),
                 )
 
         def load_words(e0, n):
@@ -81,25 +80,24 @@ def tile_routed_moe_kernel(tc, xT, w_words, w_scales, b, gate, offs, pos1, pos2,
 
         load_x(0, 0)
         load_x(0, 1)
-        nc.sync.dma_start(out=offs_t[:], in_=offs)
         load_x(0, 2)
-        nc.sync.dma_start(out=bias[:], in_=b)
-        load_x(1, 0)
-        for i in range(1, 4):
+        nc.sync.dma_start(out=offs_t[:], in_=offs)
+        for i in range(4):
             load_x(1, i)
-            load_scale_rows(i - 1, 1)
+        nc.sync.dma_start(out=bias[:], in_=b)
         for i in range(4):
             load_x(2, i)
-            load_scale_rows(3 + 2 * i, 2)
+        load_scales(0, 6)
         load_words(0, 4)
-        load_scale_rows(11, 3)
+        load_scales(6, 6)
         load_words(4, 4)
-        load_scale_rows(14, 2)
         load_words(8, 4)
         nc.sync.dma_start(out=pos1_t[:], in_=pos1)
-        load_words(12, 4)
-        nc.sync.dma_start(out=gates[0][:], in_=gate[0])
         nc.sync.dma_start(out=pos2_t[:], in_=pos2)
+        load_words(12, 2)
+        load_words(14, 1)
+        load_words(15, 1)
+        nc.sync.dma_start(out=gates[0][:], in_=gate[0])
         nc.sync.dma_start(out=gates[1][:], in_=gate[1])
 
         def quantize(a, lo, grp):
@@ -120,7 +118,7 @@ def tile_routed_moe_kernel(tc, xT, w_words, w_scales, b, gate, offs, pos1, pos2,
         x_codes = []
 
         def new_codes(a):
-            x_codes.append(ring.tile([P, T], U32, name=f"x_codes{a}", tag="x_codes", align_bytes=64))
+            x_codes.append(keep.tile([P, T], U32, name=f"x_codes{a}", align_bytes=64))
 
         new_codes(0)
         grp = [keep.tile([P, 256, 4], BF16, name=f"grp0_{i}", align_bytes=64) for i in range(4)]
@@ -138,19 +136,15 @@ def tile_routed_moe_kernel(tc, xT, w_words, w_scales, b, gate, offs, pos1, pos2,
 
         for a in (1, 2):
             new_codes(a)
-            first = ring.tile([P, 512, 4], BF16, name=f"grp{a}_first", tag=f"grp{a}", align_bytes=64)
-            third = keep.tile([P, 256, 4], BF16, name=f"grp{a}_third", align_bytes=64)
-            last_s = keep.tile([P, 128, 4], BF16, name=f"grp{a}_s", align_bytes=64)
+            first = keep.tile([P, 512, 4], BF16, name=f"grp{a}_first", align_bytes=64)
             interleave(SCA, first[:, 0:256, :], raws[a][0][:])
             interleave(SCA, first[:, 256:512, :], raws[a][1][:])
-            interleave(SCA, third[:], raws[a][2][:])
-            interleave(SCA, last_s[:], raws[a][3][:, :, 128:256])
+            rest = [keep.tile([P, 256, 4], BF16, name=f"grp{a}_{i}", align_bytes=64) for i in (2, 3)]
+            for grp_t, raw in zip(rest, raws[a][-2:]):
+                interleave(SCA, grp_t[:], raw[:])
             quantize(a, 0, first)
-            last_v = ring.tile([P, 128, 4], BF16, name=f"grp{a}_v", tag=f"grp{a}", align_bytes=64)
-            interleave(VEC, last_v[:], raws[a][3][:, :, 0:128])
-            quantize(a, 512, third)
-            quantize(a, 768, last_v)
-            quantize(a, 896, last_s)
+            quantize(a, 512, rest[0])
+            quantize(a, 768, rest[1])
             if a == 1:
                 for lo, n in ((0, 768), (768, 768), (1536, 512)):
                     gather_words(a, lo, n)
@@ -165,7 +159,7 @@ def tile_routed_moe_kernel(tc, xT, w_words, w_scales, b, gate, offs, pos1, pos2,
                 nc.tensor.matmul_mx(
                     out=accs[e][:, 0:C],
                     lhsT=w_codes[:, e * PASSES + a, :].bitcast(FP8X4),
-                    lhsT_scale=w_sc[:, e * PASSES + a, :],
+                    lhsT_scale=w_sc[4 * a : P, e, :],
                     rhs=g_codes[a][:, cols].bitcast(FP8X4),
                     rhs_scale=g_sc[4 * a : P, cols],
                     start=(a == 0),
@@ -177,19 +171,25 @@ def tile_routed_moe_kernel(tc, xT, w_words, w_scales, b, gate, offs, pos1, pos2,
             nc.scalar.activation(out=y[:, cols], in_=accs[e][:, 0:C], func=SILU, bias=bias[:, e : e + 1])
 
         for lo in (0, 768):
+            experts = range(lo // C, (lo + 768) // C)
             gather_scales(lo, 768)
+            for e in experts:
+                multiply(e, (0, 1))
             gather_words(2, lo, 768)
-            for e in range(lo // C, (lo + 768) // C):
-                multiply(e, (0, 1, 2))
-                finish(e)
-        gather_scales(1536, 512)
-        for e in range(12, 16):
-            multiply(e, (0, 1))
-        for lo, n in ((1536, 384), (1920, 128)):
-            gather_words(2, lo, n)
-            for e in range(lo // C, (lo + n) // C):
+            for e in experts:
                 multiply(e, (2,))
                 finish(e)
+        gather_scales(1536, 512)
+        for e in (12, 13, 14):
+            multiply(e, (0, 1))
+        gather_words(2, 1536, 384)
+        for e in (12, 13, 14):
+            multiply(e, (2,))
+            finish(e)
+        multiply(15, (0, 1))
+        gather_words(2, 1920, 128)
+        multiply(15, (2,))
+        finish(15)
 
         m1 = keep.tile([P, T], F32, name="m1")
         m2 = keep.tile([P, T], F32, name="m2")

from contextlib import ExitStack

import concourse.mybir as mybir

F32 = mybir.dt.float32
BF16 = mybir.dt.bfloat16
I32 = mybir.dt.int32
U32 = mybir.dt.uint32
U16 = mybir.dt.uint16
U8 = mybir.dt.uint8
FP8X4 = mybir.dt.float8_e4m3fn_x4
MULT = mybir.AluOpType.mult
ADD = mybir.AluOpType.add
SILU = mybir.ActivationFunctionType.Silu

P = 128
K, T, E, C = 1536, 1024, 16, 128
SLOTS = E * C
PASSES = 3
FLOPS = 2 * K * P * SLOTS

LOADS = [[(0, 512), (512, 256), (768, 256)], [(0, 256), (256, 256), (512, 256), (768, 256)], [(0, 256), (256, 256), (512, 256), (768, 256)]]


def offs_slice(tile, lo, n):
    return tile[:, lo // 16 : (lo + n) // 16]


def interleave(engine_copy, dst, src):
    engine_copy(out=dst.rearrange("p (c i) t -> p c t i", i=4), in_=src.rearrange("p t (c i) -> p c t i", i=4))


def tile_routed_moe_kernel(tc, xT, w_words, w_scales, b, gate, offs, pos1, pos2, out):
    nc = tc.nc
    with ExitStack() as ctx:
        keep = ctx.enter_context(tc.tile_pool(name="keep", bufs=1))
        psum = ctx.enter_context(tc.psum_pool(name="psum", bufs=8))

        offs_t = keep.tile([P, SLOTS // 16], U16, name="offs_t")
        pos1_t = keep.tile([P, T // 16], U16, name="pos1_t")
        pos2_t = keep.tile([P, T // 16], U16, name="pos2_t")
        bias = keep.tile([P, E], F32, name="bias")
        gates = [keep.tile([P, T], F32, name=f"gate{r}") for r in range(2)]
        w_codes = keep.tile([P, E * PASSES, C], U32, name="w_codes", align_bytes=64)
        w_sc = keep.tile([P, E, C], U8, name="w_sc", align_bytes=64)
        x_sc = keep.tile([P, T], U8, name="x_sc", align_bytes=64)
        g_codes = [keep.tile([P, SLOTS], U32, name=f"g_codes{a}", align_bytes=64) for a in range(PASSES)]
        g_sc = keep.tile([P, SLOTS], U8, name="g_sc", align_bytes=64)
        y = keep.tile([P, SLOTS], F32, name="y")
        warm = keep.tile([P, 1], F32, name="warm")
        warm2 = keep.tile([P, 1], F32, name="warm2")

        nc.gpsimd.memset(warm[:], 0.0)
        nc.scalar.activation(out=warm2[:], in_=warm[:], func=SILU)
        nc.gpsimd.memset(x_sc[:], 0)
        nc.gpsimd.memset(w_sc[:].rearrange("p e n -> p (e n)").bitcast(I32), 0)

        x_view = xT.rearrange("(g p t) n -> g p t n", p=P, t=4)
        raws = [[], [], []]

        def load_x(a, i):
            lo, n = LOADS[a][i]
            raw = keep.tile([P, 4, n], F32, name=f"raw{a}_{i}")
            nc.sync.dma_start(out=raw[:], in_=x_view[a, :, :, lo : lo + n])
            raws[a].append(raw)

        def load_scales(first, n):
            for a, q in [divmod(j, 4) for j in range(first, first + n)]:
                row = 32 * q + 4 * a
                nc.sync.dma_start(
                    out=w_sc[row : row + 4, :, :].bitcast(I32),
                    in_=w_scales[:, a, 4 * q : 4 * q + 4, :].rearrange("e q n -> q e n").bitcast(I32),
                )

        def load_words(e0, n):
            nc.sync.dma_start(
                out=w_codes[:, e0 * PASSES : (e0 + n) * PASSES, :].bitcast(I32),
                in_=w_words[e0 : e0 + n].rearrange("e a p n r -> p (e a) (n r)").bitcast(I32),
            )

        load_x(0, 0)
        load_x(0, 1)
        load_x(0, 2)
        nc.sync.dma_start(out=offs_t[:], in_=offs)
        for i in range(4):
            load_x(1, i)
        nc.sync.dma_start(out=bias[:], in_=b)
        for i in range(4):
            load_x(2, i)
        load_scales(0, 6)
        load_words(0, 4)
        load_scales(6, 6)
        load_words(4, 4)
        load_words(8, 4)
        nc.sync.dma_start(out=pos1_t[:], in_=pos1)
        nc.sync.dma_start(out=pos2_t[:], in_=pos2)
        load_words(12, 2)
        load_words(14, 1)
        load_words(15, 1)
        nc.sync.dma_start(out=gates[0][:], in_=gate[0])
        nc.sync.dma_start(out=gates[1][:], in_=gate[1])

        def quantize(a, lo, grp):
            n = grp.shape[1]
            nc.vector.quantize_mx(
                out=x_codes[a][:, lo : lo + n].bitcast(FP8X4),
                scales=x_sc[4 * a : P, lo : lo + n],
                in_=grp[:].rearrange("p w j -> p (w j)"),
            )

        def gather_words(a, lo, n):
            nc.vector.tensor_copy(g_codes[a][:, lo : lo + n], x_codes[a][:].indirect(offs_slice(offs_t, lo, n)))

        def gather_scales(lo, n):
            nc.vector.tensor_copy(g_sc[:, lo : lo + n], x_sc[:].indirect(offs_slice(offs_t, lo, n)))

        VEC, SCA = nc.vector.tensor_copy, nc.scalar.copy
        x_codes = []

        def new_codes(a):
            x_codes.append(keep.tile([P, T], U32, name=f"x_codes{a}", align_bytes=64))

        new_codes(0)
        grp = [keep.tile([P, 256, 4], BF16, name=f"grp0_{i}", align_bytes=64) for i in range(4)]
        interleave(VEC, grp[0][:], raws[0][0][:, :, 0:256])
        interleave(SCA, grp[1][:], raws[0][0][:, :, 256:512])
        interleave(VEC, grp[2][:], raws[0][1][:])
        quantize(0, 0, grp[0])
        quantize(0, 256, grp[1])
        interleave(SCA, grp[3][:, 160:256, :], raws[0][2][:, :, 160:256])
        interleave(VEC, grp[3][:, 0:160, :], raws[0][2][:, :, 0:160])
        quantize(0, 512, grp[2])
        quantize(0, 768, grp[3])
        for lo, n in ((0, 768), (768, 768), (1536, 512)):
            gather_words(0, lo, n)

        for a in (1, 2):
            new_codes(a)
            first = keep.tile([P, 512, 4], BF16, name=f"grp{a}_first", align_bytes=64)
            interleave(SCA, first[:, 0:256, :], raws[a][0][:])
            interleave(SCA, first[:, 256:512, :], raws[a][1][:])
            rest = [keep.tile([P, 256, 4], BF16, name=f"grp{a}_{i}", align_bytes=64) for i in (2, 3)]
            for grp_t, raw in zip(rest, raws[a][-2:]):
                interleave(SCA, grp_t[:], raw[:])
            quantize(a, 0, first)
            quantize(a, 512, rest[0])
            quantize(a, 768, rest[1])
            if a == 1:
                for lo, n in ((0, 768), (768, 768), (1536, 512)):
                    gather_words(a, lo, n)

        accs = {}

        def multiply(e, passes):
            if e not in accs:
                accs[e] = psum.tile([P, 512], F32, name="acc")
            cols = slice(e * C, (e + 1) * C)
            for a in passes:
                nc.tensor.matmul_mx(
                    out=accs[e][:, 0:C],
                    lhsT=w_codes[:, e * PASSES + a, :].bitcast(FP8X4),
                    lhsT_scale=w_sc[4 * a : P, e, :],
                    rhs=g_codes[a][:, cols].bitcast(FP8X4),
                    rhs_scale=g_sc[4 * a : P, cols],
                    start=(a == 0),
                    stop=(a == PASSES - 1),
                )

        def finish(e):
            cols = slice(e * C, (e + 1) * C)
            nc.scalar.activation(out=y[:, cols], in_=accs[e][:, 0:C], func=SILU, bias=bias[:, e : e + 1])

        for lo in (0, 768):
            experts = range(lo // C, (lo + 768) // C)
            gather_scales(lo, 768)
            for e in experts:
                multiply(e, (0, 1))
            gather_words(2, lo, 768)
            for e in experts:
                multiply(e, (2,))
                finish(e)
        gather_scales(1536, 512)
        for e in (12, 13, 14):
            multiply(e, (0, 1))
        gather_words(2, 1536, 384)
        for e in (12, 13, 14):
            multiply(e, (2,))
            finish(e)
        multiply(15, (0, 1))
        gather_words(2, 1920, 128)
        multiply(15, (2,))
        finish(15)

        m1 = keep.tile([P, T], F32, name="m1")
        m2 = keep.tile([P, T], F32, name="m2")
        res = keep.tile([P, T], F32, name="res")
        halves = ((0, 512), (512, 512))
        nc.vector.tensor_tensor(m1[:], y[:].indirect(pos1_t[:]), gates[0][:], MULT)
        for lo, n in halves:
            cols = slice(lo, lo + n)
            nc.vector.tensor_tensor(m2[:, cols], y[:].indirect(offs_slice(pos2_t, lo, n)), gates[1][:, cols], MULT)
        for lo, n in halves:
            cols = slice(lo, lo + n)
            nc.vector.tensor_tensor(res[:, cols], m1[:, cols], m2[:, cols], ADD)
            nc.sync.dma_start(out=out[:, cols], in_=res[:, cols])
